import numpy as np
import ml_dtypes


def mxq(x, axis, fmt="e4m3"):
    dtype, down = {"e4m3": (ml_dtypes.float8_e4m3fn, 7), "e5m2": (ml_dtypes.float8_e5m2, 14)}[fmt]
    v = np.moveaxis(np.asarray(x, np.float32).astype(ml_dtypes.bfloat16).astype(np.float64), axis, -1)
    blocks = v.reshape(v.shape[:-1] + (-1, 32))
    amax = np.abs(blocks).max(-1, keepdims=True)
    byte = np.maximum(np.where(amax > 0, np.frexp(amax)[1] - 1 + 127, 0) - down, 1)
    scale = np.exp2(byte - 127.0)
    codes = (blocks / scale).astype(np.float32).astype(dtype).astype(np.float64)
    return np.moveaxis((codes * scale).reshape(v.shape), -1, axis)


WIDE = False


def mx_kscale(k):
    if not WIDE:
        return np.ones(k)
    levels = np.array([30, -30])
    if k % 512:
        return np.exp2(np.random.permutation(np.resize(levels, k // 32))).repeat(32)
    a = np.empty((k // 512, 16))
    for p in range(k // 512):
        a[p, :8] = np.random.permutation(np.resize(levels, 8))
        for g in range(8):
            far = levels[np.abs(levels - a[p, g]) >= 10]
            a[p, g + 8] = far[np.random.randint(len(far))]
    return np.exp2(a.ravel()).repeat(32)


def f64(x):
    return np.asarray(x).astype(np.float64)


def striped(idx):
    return np.tile(np.asarray(idx).reshape(-1, 16).T, (8, 1)).astype(np.uint16)


def unstriped(offs):
    return offs[:16].T.reshape(-1).astype(np.int64)


E2M1 = np.array([0.0, 0.5, 1.0, 1.5, 2.0, 3.0, 4.0, 6.0, -0.0, -0.5, -1.0, -1.5, -2.0, -3.0, -4.0, -6.0])


def pack_weight(w, fmt):
    k, n = w.shape
    w = f64(np.asarray(w, np.float32).astype(ml_dtypes.bfloat16)).reshape(k // 32, 32, n)
    amax = np.abs(w).max(1)
    if fmt in ("e4m3", "e5m2"):
        byte = np.frexp(amax)[1] - 1 + 127 - (7 if fmt == "e4m3" else 14)
    else:
        mant, ex = np.frexp(amax / 6.0)
        byte = np.where(mant > 0.5, ex, ex - 1) + 127
    byte = np.clip(np.where(amax > 0, byte, 1), 1, 254)
    scaled = (w * np.exp2(127.0 - byte)[:, None, :]).reshape(k, n).astype(np.float32)
    by_word = np.ascontiguousarray(scaled.reshape(k // 512, 128, 4, n).transpose(0, 1, 3, 2))
    if fmt in ("e4m3", "e5m2"):
        words = by_word.astype(ml_dtypes.float8_e4m3fn if fmt == "e4m3" else ml_dtypes.float8_e5m2).view(np.uint8)
    else:
        c = by_word.astype(ml_dtypes.float4_e2m1fn).view(np.uint8) & 0xF
        words = (c[..., 0::2] | (c[..., 1::2] << 4)).reshape(k // 512, 128, 2 * n)
    return np.ascontiguousarray(words), np.ascontiguousarray(byte.astype(np.uint8).reshape(k // 512, 16, n))


def unpack_weight(words, scales, fmt):
    g, _, n = scales.shape
    words = np.ascontiguousarray(words).reshape(g, 128, n, -1)
    if fmt in ("e4m3", "e5m2"):
        vals = words.view(ml_dtypes.float8_e4m3fn if fmt == "e4m3" else ml_dtypes.float8_e5m2).astype(np.float64)
    else:
        nib = np.empty((g, 128, n, 4), np.uint8)
        nib[..., 0::2] = words & 0xF
        nib[..., 1::2] = words >> 4
        vals = E2M1[nib]
    vals = vals * np.repeat(np.exp2(scales.astype(np.float64) - 127.0), 8, axis=1)[..., None]
    return vals.transpose(0, 1, 3, 2).reshape(g * 512, n)


def sigmoid(v):
    return 1.0 / (1.0 + np.exp(-v))


K, T, J, R, C, N, E = 512, 2048, 256, 512, 512, 256, 1024


def setup_inputs():
    n = np.random.standard_normal
    idx = np.random.permutation(T)[:J]
    idx2 = np.random.permutation(T)[:J]
    idx3 = np.random.permutation(C)[:J]
    idx4 = np.random.permutation(C)[:J]
    idx5 = np.random.permutation(E)[:J]
    fk = mx_kscale(K)
    fr = mx_kscale(R)
    xtp = pack_weight(n((K, T)) / fk[:, None], "e5m2")
    wp = pack_weight(n((K, R)) * 1 / np.sqrt(K) * fk[:, None] * fr, "e2m1")
    wbp = pack_weight(n((R, N)) * 1 / np.sqrt(R) / fr[:, None], "e2m1")
    return {
        "xt_words": xtp[0],
        "xt_scales": xtp[1],
        "w_words": wp[0],
        "w_scales": wp[1],
        "wb_words": wbp[0],
        "wb_scales": wbp[1],
        "tz": (n((N, E))).astype(np.float32),
        "so": (np.random.uniform(0.6, 1.6, (N, 1))).astype(np.float32),
        "bo": (np.random.uniform(-1.0, 1.0, (N, 1))).astype(np.float32),
        "offs": striped(idx),
        "offs2": striped(idx2),
        "offs3": striped(idx3),
        "offs4": striped(idx4),
        "offs5": striped(idx5),
    }


def reference(xt_words, xt_scales, w_words, w_scales, wb_words, wb_scales, tz, so, bo, offs, offs2, offs3, offs4, offs5):
    idx = unstriped(offs)
    idx2 = unstriped(offs2)
    idx3 = unstriped(offs3)
    idx4 = unstriped(offs4)
    idx5 = unstriped(offs5)
    xtu = unpack_weight(xt_words, xt_scales, "e5m2")
    wu = unpack_weight(w_words, w_scales, "e2m1")
    wbu = unpack_weight(wb_words, wb_scales, "e2m1")
    xtidxg = xtu[:, idx]
    a = wu.T @ xtidxg
    xtidx2g = xtu[:, idx2]
    b = wu.T @ xtidx2g
    pw = np.zeros((R, C))
    pw[:, idx3] = a
    hid = np.abs(pw[:, idx4] - b)
    hidq = mxq(hid, 0, "e4m3")
    p = wbu.T @ hidq
    y = p * sigmoid(f64(tz)[:, idx5] * f64(so) + f64(bo))
    return y

@@ -1,0 +1,192 @@
+from contextlib import ExitStack
+
+import concourse.mybir as mybir
+
+F32 = mybir.dt.float32
+BF16 = mybir.dt.bfloat16
+I32 = mybir.dt.int32
+U32 = mybir.dt.uint32
+U16 = mybir.dt.uint16
+U8 = mybir.dt.uint8
+E4M3 = mybir.dt.float8_e4m3fn_x4
+E5M2 = mybir.dt.float8_e5m2_x4
+E2M1 = mybir.dt.float4_e2m1fn_x4
+ACT = mybir.ActivationFunctionType
+ALU = mybir.AluOpType
+
+P = 128
+PACK = 4
+K, T, J, R, C, N, E = 512, 2048, 256, 512, 512, 256, 1024
+HALF = J // 2
+FLOPS = 2 * (2 * K * R * J + R * N * J)
+
+
+def tile_list_tied_board_one_finalgate_kernel(
+    tc, xt_words, xt_scales, w_words, w_scales, wb_words, wb_scales, tz, so, bo,
+    offs, offs2, offs3, offs4, offs5, out,
+):
+    nc = tc.nc
+    with ExitStack() as ctx:
+        pool = ctx.enter_context(tc.tile_pool(name="sb", bufs=1))
+        psum = ctx.enter_context(tc.psum_pool(name="ps", bufs=1))
+
+        def sb(name, shape, dtype, tag=None):
+            return pool.tile(shape, dtype, name=name, tag=tag or name, align_bytes=64)
+
+        def load_list(name, src):
+            tile = sb(name, [P, J // 16], U16)
+            nc.sync.dma_start(tile[:], src)
+            return tile
+
+        def load_plane(name, scales, queues):
+            width = scales.shape[2]
+            plane = sb(name, [P, width], U8)
+            for q, queue in enumerate(queues):
+                rows = scales[0, 4 * q : 4 * q + 4, :].bitcast(I32)
+                queue.dma_start(
+                    plane[32 * q : 32 * (q + 1), :].bitcast(I32),
+                    rows.unsqueeze(0).broadcast_to([8, 4, width // 4]),
+                )
+            return plane
+
+        boards = [sb(f"board{t}", [P, C], F32) for t in range(PACK)]
+        for board in boards:
+            nc.vector.memset(board[:], 0.0)
+
+        x_plane = load_plane("x_plane", xt_scales, [nc.sync, nc.scalar, nc.scalar, nc.scalar])
+        list_a = load_list("list_a", offs)
+        list_b = load_list("list_b", offs2)
+        x_words = sb("x_words", [P, T], I32)
+        nc.sync.dma_start(x_words[:], xt_words[0].rearrange("p c r -> p (c r)").bitcast(I32))
+        w_raw = sb("w_raw", [P, 2 * R], U8)
+        nc.scalar.dma_start(w_raw[:].bitcast(I32), w_words[0].bitcast(I32))
+        w_plane = load_plane("w_plane", w_scales, [nc.sync, nc.sync, nc.sync, nc.sync])
+        list_put = load_list("list_put", offs3)
+        list_get = load_list("list_get", offs4)
+        list_gate = load_list("list_gate", offs5)
+        slope = sb("slope", [P, N // P], F32)
+        offset = sb("offset", [P, N // P], F32)
+        with nc.allow_non_contiguous_dma(reason="one value a partition"):
+            nc.sync.dma_start(slope[:], so.rearrange("(h p) o -> p (h o)", p=P))
+            nc.sync.dma_start(offset[:], bo.rearrange("(h p) o -> p (h o)", p=P))
+        tz_rows = []
+        for h in range(N // P):
+            rows = sb(f"tz{h}", [P, E], F32)
+            nc.sync.dma_start(rows[:], tz[h * P : (h + 1) * P, :])
+            tz_rows.append(rows)
+        wb_codes = sb("wb_codes", [P, 2 * N], U8)
+        nc.sync.dma_start(wb_codes[:].bitcast(I32), wb_words[0].bitcast(I32))
+        wb_plane = load_plane("wb_plane", wb_scales, [nc.sync, nc.sync, nc.sync, nc.sync])
+
+
+        picked = []
+        for name, lst in (("a", list_a), ("b", list_b)):
+            scl = sb(f"xs_{name}", [P, J], U8)
+            nc.vector.tensor_copy(scl[:], x_plane[:].indirect(lst[:]))
+            picked.append(scl)
+
+        w_codes = sb("w_codes", [P, 2 * R], U8)
+        w_dealt = sb("w_dealt", [P, R], U8)
+        nc.vector.tensor_copy(
+            w_codes[:].bitcast(U16).rearrange("p (t m) -> p t m", t=PACK),
+            w_raw[:].bitcast(U16).rearrange("p (m t) -> p t m", t=PACK),
+        )
+        words = [sb(f"xw_{name}", [P, J], U32) for name in "ab"]
+        nc.vector.tensor_copy(words[0][:], x_words[:].bitcast(U32).indirect(list_a[:]))
+        nc.vector.tensor_copy(
+            w_dealt[:].rearrange("p (t m) -> p t m", t=PACK),
+            w_plane[:].rearrange("p (m t) -> p t m", t=PACK),
+        )
+        nc.vector.tensor_copy(words[1][:], x_words[:].bitcast(U32).indirect(list_b[:]))
+
+        def first_product(dst, t, side, cols):
+            nc.tensor.matmul_mx(
+                dst,
+                lhsT=w_codes[:, 2 * P * t : 2 * P * (t + 1)].bitcast(E2M1),
+                lhsT_scale=w_dealt[:, P * t : P * (t + 1)],
+                rhs=words[side][:, cols].bitcast(E5M2),
+                rhs_scale=picked[side][:, cols],
+                start=True,
+                stop=True,
+            )
+
+        halves = [slice(u * HALF, (u + 1) * HALF) for u in range(2)]
+        a_ps = [psum.tile([P, J], F32, name=f"a_ps{t}", tag=f"bank{t}") for t in range(PACK)]
+        b_ps = [psum.tile([P, PACK, HALF], F32, name=f"b_ps{u}") for u in range(2)]
+        for t in range(PACK):
+            first_product(a_ps[t][:], t, 0, slice(0, J))
+        for u in range(2):
+            for t in range(PACK):
+                first_product(b_ps[u][:, t, :], t, 1, halves[u])
+
+        a_sb = [sb(f"a_sb{t}", [P, J], F32) for t in range(PACK)]
+        for t in (0, 1):
+            nc.scalar.copy(a_sb[t][:], a_ps[t][:])
+        for t in (2, 3):
+            nc.vector.tensor_copy(a_sb[t][:], a_ps[t][:])
+        for t in (0, 1):
+            nc.scalar.activation(boards[t][:].indirect(list_put[:]), a_sb[t][:], ACT.Copy)
+        for t in (2, 3):
+            nc.vector.tensor_copy(boards[t][:].indirect(list_put[:]), a_sb[t][:])
+
+        def look(h):
+            gate = sb(f"gate{h}", [P, J], F32, tag=("a_sb1", "diff1")[h])
+            nc.scalar.activation(
+                gate[:], tz_rows[h][:].indirect(list_gate[:]), ACT.Sigmoid,
+                bias=offset[:, h : h + 1], scale=slope[:, h : h + 1],
+            )
+            return gate
+
+        def difference(u):
+            got = [sb(f"got_low{u}", [P, 2, HALF], F32), sb(f"got_high{u}", [P, 2, HALF], F32, tag="got_high")]
+            diff = sb(f"diff{u}", [P, PACK, HALF], F32)
+            entries = list_get[:, u * HALF // 16 : (u + 1) * HALF // 16]
+            for t in range(PACK):
+                if t < 2:
+                    nc.scalar.activation(got[t // 2][:, t % 2, :], boards[t][:].indirect(entries), ACT.Copy)
+                else:
+                    nc.vector.tensor_copy(got[t // 2][:, t % 2, :], boards[t][:].indirect(entries))
+            for v in range(2):
+                pair = slice(2 * v, 2 * v + 2)
+                nc.vector.tensor_tensor(diff[:, pair, :], got[v][:], b_ps[u][:, pair, :], ALU.subtract)
+            return diff
+
+        def magnitude(u, diff):
+            hid = sb(f"hid{u}", [P, HALF, PACK], BF16)
+            nc.scalar.activation(hid[:], diff[:].rearrange("p t j -> p j t"), ACT.Abs)
+            return hid
+
+        ys = [sb(f"y{h}", [P, J], F32) for h in range(N // P)]
+
+        def second_product(u, hid):
+            codes = sb(f"hid_codes{u}", [P, HALF], U32)
+            plane = sb(f"hid_plane{u}", [P, HALF], U8)
+            nc.vector.quantize_mx(
+                out=codes[:].bitcast(E4M3),
+                scales=plane[:],
+                in_=hid[:].rearrange("p j t -> p (j t)"),
+            )
+            sums = []
+            for h in range(N // P):
+                p_ps = psum.tile([P, HALF], F32, name=f"p_ps{u}{h}", tag=f"bank{2 * u + h}")
+                nc.tensor.matmul_mx(
+                    p_ps[:],
+                    lhsT=wb_codes[:, 2 * P * h : 2 * P * (h + 1)].bitcast(E2M1),
+                    lhsT_scale=wb_plane[:, P * h : P * (h + 1)],
+                    rhs=codes[:].bitcast(E4M3),
+                    rhs_scale=plane[:],
+                    start=True,
+                    stop=True,
+                )
+                sums.append(p_ps)
+            return sums
+
+        diffs = [difference(u) for u in range(2)]
+        gates = [look(0)]
+        hids = [magnitude(u, diffs[u]) for u in range(2)]
+        gates.append(look(1))
+        sums = [second_product(u, hids[u]) for u in range(2)]
+        for h in range(N // P):
+            for u in range(2):
+                nc.vector.tensor_tensor(ys[h][:, halves[u]], sums[u][h][:], gates[h][:, halves[u]], ALU.mult)
+            nc.sync.dma_start(out[h * P : (h + 1) * P, :], ys[h][:])

@@ -78,6 +78,9 @@ def tile_list_tied_board_one_finalgate_kernel(
         nc.sync.dma_start(wb_codes[:].bitcast(I32), wb_words[0].bitcast(I32))
         wb_plane = load_plane("wb_plane", wb_scales, [nc.sync, nc.sync, nc.sync, nc.sync])
 
+        warm = sb("warm", [P, 1], F32)
+        nc.vector.memset(warm[:], 0.0)
+        nc.scalar.activation(warm[:], warm[:], ACT.Sigmoid)
 
         picked = []
         for name, lst in (("a", list_a), ("b", list_b)):

@@ -38,29 +38,35 @@ def tile_list_tied_board_one_finalgate_kernel(
             nc.sync.dma_start(tile[:], src)
             return tile
 
-        def load_plane(name, scales, queues):
-            width = scales.shape[2]
+        def clear_plane(name, width):
             plane = sb(name, [P, width], U8)
-            for q, queue in enumerate(queues):
-                rows = scales[0, 4 * q : 4 * q + 4, :].bitcast(I32)
-                queue.dma_start(
-                    plane[32 * q : 32 * (q + 1), :].bitcast(I32),
-                    rows.unsqueeze(0).broadcast_to([8, 4, width // 4]),
-                )
+            nc.vector.memset(plane[:].bitcast(I32), 0)
             return plane
 
+        def load_plane(plane, scales, queues):
+            for q, queue in enumerate(queues):
+                queue.dma_start(
+                    plane[32 * q : 32 * q + 4, :].bitcast(I32),
+                    scales[0, 4 * q : 4 * q + 4, :].bitcast(I32),
+                )
+
+        x_plane = sb("x_plane", [P, T], U8)
+        nc.vector.memset(x_plane[:, : T // 2].bitcast(I32), 0)
+        nc.gpsimd.memset(x_plane[:, T // 2 :].bitcast(I32), 0)
+        w_plane = clear_plane("w_plane", R)
+        wb_plane = clear_plane("wb_plane", N)
         boards = [sb(f"board{t}", [P, C], F32) for t in range(PACK)]
         for board in boards:
             nc.vector.memset(board[:], 0.0)
 
-        x_plane = load_plane("x_plane", xt_scales, [nc.sync, nc.scalar, nc.scalar, nc.scalar])
         list_a = load_list("list_a", offs)
         list_b = load_list("list_b", offs2)
+        w_raw = sb("w_raw", [P, 2 * R], U8)
+        nc.sync.dma_start(w_raw[:].bitcast(I32), w_words[0].bitcast(I32))
+        load_plane(x_plane, xt_scales, [nc.sync, nc.sync, nc.scalar, nc.scalar])
         x_words = sb("x_words", [P, T], I32)
         nc.sync.dma_start(x_words[:], xt_words[0].rearrange("p c r -> p (c r)").bitcast(I32))
-        w_raw = sb("w_raw", [P, 2 * R], U8)
-        nc.scalar.dma_start(w_raw[:].bitcast(I32), w_words[0].bitcast(I32))
-        w_plane = load_plane("w_plane", w_scales, [nc.sync, nc.sync, nc.sync, nc.sync])
+        load_plane(w_plane, w_scales, [nc.sync, nc.sync, nc.sync, nc.sync])
         list_put = load_list("list_put", offs3)
         list_get = load_list("list_get", offs4)
         list_gate = load_list("list_gate", offs5)
@@ -76,7 +82,7 @@ def tile_list_tied_board_one_finalgate_kernel(
             tz_rows.append(rows)
         wb_codes = sb("wb_codes", [P, 2 * N], U8)
         nc.sync.dma_start(wb_codes[:].bitcast(I32), wb_words[0].bitcast(I32))
-        wb_plane = load_plane("wb_plane", wb_scales, [nc.sync, nc.sync, nc.sync, nc.sync])
+        load_plane(wb_plane, wb_scales, [nc.sync, nc.sync, nc.sync, nc.sync])
 
         warm = sb("warm", [P, 1], F32)
         nc.vector.memset(warm[:], 0.0)
@@ -94,7 +100,7 @@ def tile_list_tied_board_one_finalgate_kernel(
             w_codes[:].bitcast(U16).rearrange("p (t m) -> p t m", t=PACK),
             w_raw[:].bitcast(U16).rearrange("p (m t) -> p t m", t=PACK),
         )
-        words = [sb(f"xw_{name}", [P, J], U32) for name in "ab"]
+        words = [sb("xw_a", [P, J], U32), sb("xw_b", [P, J], U32, tag="w_plane")]
         nc.vector.tensor_copy(words[0][:], x_words[:].bitcast(U32).indirect(list_a[:]))
         nc.vector.tensor_copy(
             w_dealt[:].rearrange("p (t m) -> p t m", t=PACK),
@@ -133,7 +139,7 @@ def tile_list_tied_board_one_finalgate_kernel(
             nc.vector.tensor_copy(boards[t][:].indirect(list_put[:]), a_sb[t][:])
 
         def look(h):
-            gate = sb(f"gate{h}", [P, J], F32, tag=("a_sb1", "diff1")[h])
+            gate = sb(f"gate{h}", [P, J], F32, tag=("a_sb1", "diff0")[h])
             nc.scalar.activation(
                 gate[:], tz_rows[h][:].indirect(list_gate[:]), ACT.Sigmoid,
                 bias=offset[:, h : h + 1], scale=slope[:, h : h + 1],
@@ -155,11 +161,17 @@ def tile_list_tied_board_one_finalgate_kernel(
             return diff
 
         def magnitude(u, diff):
-            hid = sb(f"hid{u}", [P, HALF, PACK], BF16)
-            nc.scalar.activation(hid[:], diff[:].rearrange("p t j -> p j t"), ACT.Abs)
+            hid = sb(f"hid{u}", [P, HALF, PACK], BF16, tag=f"tz{u}")
+            on_scalar = HALF if u == 0 else HALF - 64
+            nc.scalar.activation(
+                hid[:, :on_scalar, :].rearrange("p (c i) t -> p c t i", i=4),
+                diff[:, :, :on_scalar].rearrange("p t (c i) -> p c t i", i=4),
+                ACT.Abs,
+            )
+            if on_scalar < HALF:
+                rest = diff[:, :, on_scalar:].rearrange("p t j -> p j t")
+                nc.vector.scalar_tensor_tensor(hid[:, on_scalar:, :], rest, -1.0, rest, ALU.mult, ALU.max)
             return hid
-
-        ys = [sb(f"y{h}", [P, J], F32) for h in range(N // P)]
 
         def second_product(u, hid):
             codes = sb(f"hid_codes{u}", [P, HALF], U32)
@@ -185,11 +197,13 @@ def tile_list_tied_board_one_finalgate_kernel(
             return sums
 
         diffs = [difference(u) for u in range(2)]
-        gates = [look(0)]
-        hids = [magnitude(u, diffs[u]) for u in range(2)]
-        gates.append(look(1))
+        gates, hids = [], []
+        for u in range(2):
+            gates.append(look(u))
+            hids.append(magnitude(u, diffs[u]))
         sums = [second_product(u, hids[u]) for u in range(2)]
-        for h in range(N // P):
-            for u in range(2):
-                nc.vector.tensor_tensor(ys[h][:, halves[u]], sums[u][h][:], gates[h][:, halves[u]], ALU.mult)
-            nc.sync.dma_start(out[h * P : (h + 1) * P, :], ys[h][:])
+        for u in range(2):
+            for h in range(N // P):
+                y = sb(f"y{u}{h}", [P, HALF], F32)
+                nc.vector.tensor_tensor(y[:], sums[u][h][:], gates[h][:, halves[u]], ALU.mult)
+                nc.sync.dma_start(out[h * P : (h + 1) * P, halves[u]], y[:])

from contextlib import ExitStack

import concourse.mybir as mybir

F32 = mybir.dt.float32
BF16 = mybir.dt.bfloat16
I32 = mybir.dt.int32
U32 = mybir.dt.uint32
U16 = mybir.dt.uint16
U8 = mybir.dt.uint8
E4M3 = mybir.dt.float8_e4m3fn_x4
E5M2 = mybir.dt.float8_e5m2_x4
E2M1 = mybir.dt.float4_e2m1fn_x4
ACT = mybir.ActivationFunctionType
ALU = mybir.AluOpType

P = 128
PACK = 4
K, T, J, R, C, N, E = 512, 2048, 256, 512, 512, 256, 1024
HALF = J // 2
FLOPS = 2 * (2 * K * R * J + R * N * J)


def tile_list_tied_board_one_finalgate_kernel(
    tc, xt_words, xt_scales, w_words, w_scales, wb_words, wb_scales, tz, so, bo,
    offs, offs2, offs3, offs4, offs5, out,
):
    nc = tc.nc
    with ExitStack() as ctx:
        pool = ctx.enter_context(tc.tile_pool(name="sb", bufs=1))
        psum = ctx.enter_context(tc.psum_pool(name="ps", bufs=1))

        def sb(name, shape, dtype, tag=None):
            return pool.tile(shape, dtype, name=name, tag=tag or name, align_bytes=64)

        def load_list(name, src):
            tile = sb(name, [P, J // 16], U16)
            nc.sync.dma_start(tile[:], src)
            return tile

        def clear_plane(name, width):
            plane = sb(name, [P, width], U8)
            nc.vector.memset(plane[:].bitcast(I32), 0)
            return plane

        def load_plane(plane, scales, queues):
            for q, queue in enumerate(queues):
                queue.dma_start(
                    plane[32 * q : 32 * q + 4, :].bitcast(I32),
                    scales[0, 4 * q : 4 * q + 4, :].bitcast(I32),
                )

        x_plane = sb("x_plane", [P, T], U8)
        nc.vector.memset(x_plane[:, : T // 2].bitcast(I32), 0)
        nc.gpsimd.memset(x_plane[:, T // 2 :].bitcast(I32), 0)
        w_plane = clear_plane("w_plane", R)
        wb_plane = clear_plane("wb_plane", N)
        boards = [sb(f"board{t}", [P, C], F32) for t in range(PACK)]
        for board in boards:
            nc.vector.memset(board[:], 0.0)

        list_a = load_list("list_a", offs)
        list_b = load_list("list_b", offs2)
        w_raw = sb("w_raw", [P, 2 * R], U8)
        nc.sync.dma_start(w_raw[:].bitcast(I32), w_words[0].bitcast(I32))
        load_plane(x_plane, xt_scales, [nc.sync, nc.sync, nc.scalar, nc.scalar])
        x_words = sb("x_words", [P, T], I32)
        nc.sync.dma_start(x_words[:], xt_words[0].rearrange("p c r -> p (c r)").bitcast(I32))
        load_plane(w_plane, w_scales, [nc.sync, nc.sync, nc.sync, nc.sync])
        list_put = load_list("list_put", offs3)
        list_get = load_list("list_get", offs4)
        list_gate = load_list("list_gate", offs5)
        slope = sb("slope", [P, N // P], F32)
        offset = sb("offset", [P, N // P], F32)
        with nc.allow_non_contiguous_dma(reason="one value a partition"):
            nc.sync.dma_start(slope[:], so.rearrange("(h p) o -> p (h o)", p=P))
            nc.sync.dma_start(offset[:], bo.rearrange("(h p) o -> p (h o)", p=P))
        tz_rows = []
        for h in range(N // P):
            rows = sb(f"tz{h}", [P, E], F32)
            nc.sync.dma_start(rows[:], tz[h * P : (h + 1) * P, :])
            tz_rows.append(rows)
        wb_codes = sb("wb_codes", [P, 2 * N], U8)
        nc.sync.dma_start(wb_codes[:].bitcast(I32), wb_words[0].bitcast(I32))
        load_plane(wb_plane, wb_scales, [nc.sync, nc.sync, nc.sync, nc.sync])

        warm = sb("warm", [P, 1], F32)
        nc.vector.memset(warm[:], 0.0)
        nc.scalar.activation(warm[:], warm[:], ACT.Sigmoid)

        picked = []
        for name, lst in (("a", list_a), ("b", list_b)):
            scl = sb(f"xs_{name}", [P, J], U8)
            nc.vector.tensor_copy(scl[:], x_plane[:].indirect(lst[:]))
            picked.append(scl)

        w_codes = sb("w_codes", [P, 2 * R], U8)
        w_dealt = sb("w_dealt", [P, R], U8)
        nc.vector.tensor_copy(
            w_codes[:].bitcast(U16).rearrange("p (t m) -> p t m", t=PACK),
            w_raw[:].bitcast(U16).rearrange("p (m t) -> p t m", t=PACK),
        )
        words = [sb("xw_a", [P, J], U32), sb("xw_b", [P, J], U32, tag="w_plane")]
        nc.vector.tensor_copy(words[0][:], x_words[:].bitcast(U32).indirect(list_a[:]))
        nc.vector.tensor_copy(
            w_dealt[:].rearrange("p (t m) -> p t m", t=PACK),
            w_plane[:].rearrange("p (m t) -> p t m", t=PACK),
        )
        nc.vector.tensor_copy(words[1][:], x_words[:].bitcast(U32).indirect(list_b[:]))

        def first_product(dst, t, side, cols):
            nc.tensor.matmul_mx(
                dst,
                lhsT=w_codes[:, 2 * P * t : 2 * P * (t + 1)].bitcast(E2M1),
                lhsT_scale=w_dealt[:, P * t : P * (t + 1)],
                rhs=words[side][:, cols].bitcast(E5M2),
                rhs_scale=picked[side][:, cols],
                start=True,
                stop=True,
            )

        halves = [slice(u * HALF, (u + 1) * HALF) for u in range(2)]
        a_ps = [psum.tile([P, J], F32, name=f"a_ps{t}", tag=f"bank{t}") for t in range(PACK)]
        b_ps = [psum.tile([P, PACK, HALF], F32, name=f"b_ps{u}") for u in range(2)]
        for t in range(PACK):
            first_product(a_ps[t][:], t, 0, slice(0, J))
        for u in range(2):
            for t in range(PACK):
                first_product(b_ps[u][:, t, :], t, 1, halves[u])

        a_sb = [sb(f"a_sb{t}", [P, J], F32) for t in range(PACK)]
        for t in (0, 1):
            nc.scalar.copy(a_sb[t][:], a_ps[t][:])
        for t in (2, 3):
            nc.vector.tensor_copy(a_sb[t][:], a_ps[t][:])
        for t in (0, 1):
            nc.scalar.activation(boards[t][:].indirect(list_put[:]), a_sb[t][:], ACT.Copy)
        for t in (2, 3):
            nc.vector.tensor_copy(boards[t][:].indirect(list_put[:]), a_sb[t][:])

        def look(h):
            gate = sb(f"gate{h}", [P, J], F32, tag=("a_sb1", "diff0")[h])
            nc.scalar.activation(
                gate[:], tz_rows[h][:].indirect(list_gate[:]), ACT.Sigmoid,
                bias=offset[:, h : h + 1], scale=slope[:, h : h + 1],
            )
            return gate

        def difference(u):
            got = [sb(f"got_low{u}", [P, 2, HALF], F32), sb(f"got_high{u}", [P, 2, HALF], F32, tag="got_high")]
            diff = sb(f"diff{u}", [P, PACK, HALF], F32)
            entries = list_get[:, u * HALF // 16 : (u + 1) * HALF // 16]
            for t in range(PACK):
                if t < 2:
                    nc.scalar.activation(got[t // 2][:, t % 2, :], boards[t][:].indirect(entries), ACT.Copy)
                else:
                    nc.vector.tensor_copy(got[t // 2][:, t % 2, :], boards[t][:].indirect(entries))
            for v in range(2):
                pair = slice(2 * v, 2 * v + 2)
                nc.vector.tensor_tensor(diff[:, pair, :], got[v][:], b_ps[u][:, pair, :], ALU.subtract)
            return diff

        def magnitude(u, diff):
            hid = sb(f"hid{u}", [P, HALF, PACK], BF16, tag=f"tz{u}")
            on_scalar = HALF if u == 0 else HALF - 64
            nc.scalar.activation(
                hid[:, :on_scalar, :].rearrange("p (c i) t -> p c t i", i=4),
                diff[:, :, :on_scalar].rearrange("p t (c i) -> p c t i", i=4),
                ACT.Abs,
            )
            if on_scalar < HALF:
                rest = diff[:, :, on_scalar:].rearrange("p t j -> p j t")
                nc.vector.scalar_tensor_tensor(hid[:, on_scalar:, :], rest, -1.0, rest, ALU.mult, ALU.max)
            return hid

        def second_product(u, hid):
            codes = sb(f"hid_codes{u}", [P, HALF], U32)
            plane = sb(f"hid_plane{u}", [P, HALF], U8)
            nc.vector.quantize_mx(
                out=codes[:].bitcast(E4M3),
                scales=plane[:],
                in_=hid[:].rearrange("p j t -> p (j t)"),
            )
            sums = []
            for h in range(N // P):
                p_ps = psum.tile([P, HALF], F32, name=f"p_ps{u}{h}", tag=f"bank{2 * u + h}")
                nc.tensor.matmul_mx(
                    p_ps[:],
                    lhsT=wb_codes[:, 2 * P * h : 2 * P * (h + 1)].bitcast(E2M1),
                    lhsT_scale=wb_plane[:, P * h : P * (h + 1)],
                    rhs=codes[:].bitcast(E4M3),
                    rhs_scale=plane[:],
                    start=True,
                    stop=True,
                )
                sums.append(p_ps)
            return sums

        diffs = [difference(u) for u in range(2)]
        gates, hids = [], []
        for u in range(2):
            gates.append(look(u))
            hids.append(magnitude(u, diffs[u]))
        sums = [second_product(u, hids[u]) for u in range(2)]
        for u in range(2):
            for h in range(N // P):
                y = sb(f"y{u}{h}", [P, HALF], F32)
                nc.vector.tensor_tensor(y[:], sums[u][h][:], gates[h][:, halves[u]], ALU.mult)
                nc.sync.dma_start(out[h * P : (h + 1) * P, halves[u]], y[:])
